import numpy as np
import ml_dtypes

BF16 = ml_dtypes.bfloat16


def bf(x):
    return np.asarray(x, np.float32).astype(BF16)


def f32(x):
    return np.asarray(x, np.float32)


def f64(x):
    return np.asarray(x).astype(np.float64)


def striped(idx):
    return np.concatenate([l.reshape(-1, 16).T for l in idx])


def rows(idx, k):
    return np.tile(np.repeat(idx, 16, axis=0), (k // (16 * 8), 1))


def look(tab, idx):
    return np.take_along_axis(f64(tab), rows(idx, len(tab)), axis=1)


K, S, H, D, V, N, M = 128, 2048, 256, 3, 512, 1536, 256


def setup_inputs():
    return {"z": bf(np.random.standard_normal((H, S))), "wt": bf(np.random.standard_normal((H, K)) / np.sqrt(H)), "u0": f32(np.random.uniform(0.2, 1.0, (K, V))), "u1": f32(np.random.uniform(0.2, 1.0, (K, V))), "u2": f32(np.random.uniform(0.2, 1.0, (K, V))), "w": bf(np.random.standard_normal((K, M)) / np.sqrt(K)), "b": f32(0.5 * np.random.standard_normal((M, 1))), "offs": striped(np.stack([np.random.permutation(S)[:N] for _ in range(8)]))}


def reference(z, wt, u0, u1, u2, w, b, offs):
    idx = np.stack([g.T.reshape(-1) for g in np.split(offs, 8)])
    tab = f64(wt).T @ f64(z)
    x = f64(u0) * look(tab, idx[:, :V]) + f64(u1) * look(tab, idx[:, 1 * V:2 * V]) + f64(u2) * look(tab, idx[:, 2 * V:3 * V])
    return np.maximum(f64(w).T @ x + f64(b), 0.0)

@@ -1,0 +1,79 @@
+import concourse.mybir as mybir
+
+BF16, F32, U16 = mybir.dt.bfloat16, mybir.dt.float32, mybir.dt.uint16
+ADD, MULT, MAX = mybir.AluOpType.add, mybir.AluOpType.mult, mybir.AluOpType.max
+RELU = mybir.ActivationFunctionType.Relu
+
+P = 128
+S = 2048
+H = 256
+V = 512
+D = 3
+M = 256
+BANK = 512
+OFFSET_COLUMNS = V // 16
+
+FLOPS = 2 * P * H * S + 2 * P * M * V
+
+
+def tile_lookup_pjmix_relu_kernel(tc, z, wt, u0, u1, u2, w, b, offs, out):
+    nc = tc.nc
+    halves = H // P
+    blocks = M // P
+    with (
+        tc.tile_pool(name="held", bufs=1) as held,
+        tc.psum_pool(name="projected", bufs=4) as projected_pool,
+        tc.psum_pool(name="layer", bufs=2) as layer_pool,
+    ):
+        wt_tile = held.tile([P, halves, P], BF16, name="wt_tile")
+        z_tiles = [held.tile([P, halves, BANK], BF16, name=f"z_tile{c}") for c in range(S // BANK)]
+        offsets = held.tile([P, D * OFFSET_COLUMNS], U16, name="offsets")
+        u_tiles = [held.tile([P, V], F32, name=f"u_tile{d}") for d in range(D)]
+        w_tile = held.tile([P, M], BF16, name="w_tile")
+        bias = held.tile([P, blocks], F32, name="bias")
+
+        nc.sync.dma_start(wt_tile[:], wt.rearrange("(p h) r -> p h r", h=halves))
+        z_by_partition = z.rearrange("(p h) i -> p h i", h=halves)
+        for c, z_tile in enumerate(z_tiles):
+            nc.sync.dma_start(z_tile[:], z_by_partition[:, :, c * BANK : (c + 1) * BANK])
+        nc.sync.dma_start(offsets[:], offs)
+        for u_tile, u in zip(u_tiles, (u0, u1, u2)):
+            nc.sync.dma_start(u_tile[:], u)
+        nc.sync.dma_start(w_tile[:], w)
+        nc.gpsimd.dma_start(bias[:], b.rearrange("(p h) o -> p (h o)", h=blocks))
+
+        table = held.tile([P, S], F32, name="table")
+        for c, z_tile in enumerate(z_tiles):
+            projected = projected_pool.tile([P, BANK], F32, name="projected")
+            for h in range(halves):
+                nc.tensor.matmul(
+                    projected[:], wt_tile[:, h, :], z_tile[:, h, :], start=h == 0, stop=h == halves - 1
+                )
+            columns = table[:, c * BANK : (c + 1) * BANK]
+            if c % 2 == 0:
+                nc.scalar.copy(columns, projected[:])
+            else:
+                nc.vector.tensor_copy(columns, projected[:])
+
+        products = [held.tile([P, V], F32, name=f"product{d}") for d in range(D)]
+        for d in range(D):
+            piece = offsets[:, d * OFFSET_COLUMNS : (d + 1) * OFFSET_COLUMNS]
+            nc.vector.tensor_tensor(products[d][:], table[:].indirect(piece), u_tiles[d][:], MULT)
+
+        partial = held.tile([P, V], F32, name="partial")
+        x = held.tile([P, V], BF16, name="x")
+        nc.vector.tensor_tensor(partial[:], products[0][:], products[1][:], ADD)
+        nc.vector.tensor_tensor(x[:], partial[:], products[2][:], ADD)
+
+        out_by_partition = out.rearrange("(p h) j -> p h j", h=blocks)
+        w_by_block = w_tile[:].rearrange("r (p h) -> r h p", h=blocks)
+        for h in range(blocks):
+            layer = layer_pool.tile([P, V], F32, name="layer")
+            nc.tensor.matmul(layer[:], w_by_block[:, h, :], x[:], start=True, stop=True)
+            result = held.tile([P, V], F32, name=f"result{h}")
+            if h % 2 == 0:
+                nc.scalar.activation(result[:], layer[:], RELU, bias=bias[:, h : h + 1])
+                nc.scalar.dma_start(out_by_partition[:, h, :], result[:])
+            else:
+                nc.vector.tensor_scalar(result[:], layer[:], bias[:, h : h + 1], 0.0, ADD, MAX)
+                nc.sync.dma_start(out_by_partition[:, h, :], result[:])

@@ -11,69 +11,91 @@ V = 512
 D = 3
 M = 256
 BANK = 512
-OFFSET_COLUMNS = V // 16
+FEATURES = H // P
+ROWS = M // P
+CHUNKS = S // BANK
+PIECES = (V // 2, V // 4, V // 4)
 
 FLOPS = 2 * P * H * S + 2 * P * M * V
 
 
 def tile_lookup_pjmix_relu_kernel(tc, z, wt, u0, u1, u2, w, b, offs, out):
     nc = tc.nc
-    halves = H // P
-    blocks = M // P
     with (
         tc.tile_pool(name="held", bufs=1) as held,
+        tc.psum_pool(name="scratch", bufs=1) as scratch_pool,
         tc.psum_pool(name="projected", bufs=4) as projected_pool,
-        tc.psum_pool(name="layer", bufs=2) as layer_pool,
+        tc.psum_pool(name="layer", bufs=3) as layer_pool,
     ):
-        wt_tile = held.tile([P, halves, P], BF16, name="wt_tile")
-        z_tiles = [held.tile([P, halves, BANK], BF16, name=f"z_tile{c}") for c in range(S // BANK)]
-        offsets = held.tile([P, D * OFFSET_COLUMNS], U16, name="offsets")
+        wt_tile = held.tile([P, FEATURES, P], BF16, name="wt_tile")
+        z_tiles = [held.tile([P, FEATURES, BANK], BF16, name=f"z_tile{c}") for c in range(CHUNKS)]
+        offsets = held.tile([P, D * V // 16], U16, name="offsets")
         u_tiles = [held.tile([P, V], F32, name=f"u_tile{d}") for d in range(D)]
         w_tile = held.tile([P, M], BF16, name="w_tile")
-        bias = held.tile([P, blocks], F32, name="bias")
+        bias = held.tile([P, ROWS], F32, name="bias")
 
-        nc.sync.dma_start(wt_tile[:], wt.rearrange("(p h) r -> p h r", h=halves))
-        z_by_partition = z.rearrange("(p h) i -> p h i", h=halves)
+        nc.sync.dma_start(wt_tile[:], wt.rearrange("(p k) r -> p k r", k=FEATURES))
+        z_by_partition = z.rearrange("(p k) i -> p k i", k=FEATURES)
         for c, z_tile in enumerate(z_tiles):
             nc.sync.dma_start(z_tile[:], z_by_partition[:, :, c * BANK : (c + 1) * BANK])
         nc.sync.dma_start(offsets[:], offs)
         for u_tile, u in zip(u_tiles, (u0, u1, u2)):
             nc.sync.dma_start(u_tile[:], u)
         nc.sync.dma_start(w_tile[:], w)
-        nc.gpsimd.dma_start(bias[:], b.rearrange("(p h) o -> p (h o)", h=blocks))
+        nc.sync.dma_start(bias[:], b.rearrange("(p m) o -> p (m o)", m=ROWS))
 
+        zeros = held.tile([P, BANK], BF16, name="zeros")
+        nc.vector.memset(zeros[:], 0.0)
+        scratch = scratch_pool.tile([P, BANK], F32, name="scratch")
+        for c in range(CHUNKS):
+            nc.tensor.matmul(scratch[:], zeros[:, :P], zeros[:], start=True, stop=True)
+
+        steps = [(c, 0, BANK) for c in range(CHUNKS - 1)]
+        steps += [(CHUNKS - 1, 0, BANK // 2), (CHUNKS - 1, BANK // 2, BANK // 2)]
         table = held.tile([P, S], F32, name="table")
-        for c, z_tile in enumerate(z_tiles):
-            projected = projected_pool.tile([P, BANK], F32, name="projected")
-            for h in range(halves):
+        for step, (c, start, width) in enumerate(steps):
+            projected = projected_pool.tile([P, width], F32, name="projected")
+            for k in range(FEATURES):
                 nc.tensor.matmul(
-                    projected[:], wt_tile[:, h, :], z_tile[:, h, :], start=h == 0, stop=h == halves - 1
+                    projected[:],
+                    wt_tile[:, k, :],
+                    z_tiles[c][:, k, start : start + width],
+                    start=k == 0,
+                    stop=k == FEATURES - 1,
                 )
-            columns = table[:, c * BANK : (c + 1) * BANK]
-            if c % 2 == 0:
+            columns = table[:, c * BANK + start : c * BANK + start + width]
+            if step % 2 == 0:
                 nc.scalar.copy(columns, projected[:])
             else:
                 nc.vector.tensor_copy(columns, projected[:])
 
-        products = [held.tile([P, V], F32, name=f"product{d}") for d in range(D)]
-        for d in range(D):
-            piece = offsets[:, d * OFFSET_COLUMNS : (d + 1) * OFFSET_COLUMNS]
-            nc.vector.tensor_tensor(products[d][:], table[:].indirect(piece), u_tiles[d][:], MULT)
+        out_by_partition = out.rearrange("(p m) j -> p m j", m=ROWS)
+        w_by_row = w_tile[:].rearrange("r (p m) -> r m p", m=ROWS)
+        first = 0
+        for piece, width in enumerate(PIECES):
+            j = slice(first, first + width)
 
-        partial = held.tile([P, V], F32, name="partial")
-        x = held.tile([P, V], BF16, name="x")
-        nc.vector.tensor_tensor(partial[:], products[0][:], products[1][:], ADD)
-        nc.vector.tensor_tensor(x[:], partial[:], products[2][:], ADD)
+            products = []
+            for d in range(D):
+                entry = V * d + first
+                listed = table[:].indirect(offsets[:, entry // 16 : (entry + width) // 16])
+                product = held.tile([P, width], F32, name=f"product{d}_{piece}")
+                nc.vector.tensor_tensor(product[:], listed, u_tiles[d][:, j], MULT)
+                products.append(product)
 
-        out_by_partition = out.rearrange("(p h) j -> p h j", h=blocks)
-        w_by_block = w_tile[:].rearrange("r (p h) -> r h p", h=blocks)
-        for h in range(blocks):
-            layer = layer_pool.tile([P, V], F32, name="layer")
-            nc.tensor.matmul(layer[:], w_by_block[:, h, :], x[:], start=True, stop=True)
-            result = held.tile([P, V], F32, name=f"result{h}")
-            if h % 2 == 0:
-                nc.scalar.activation(result[:], layer[:], RELU, bias=bias[:, h : h + 1])
-                nc.scalar.dma_start(out_by_partition[:, h, :], result[:])
-            else:
-                nc.vector.tensor_scalar(result[:], layer[:], bias[:, h : h + 1], 0.0, ADD, MAX)
-                nc.sync.dma_start(out_by_partition[:, h, :], result[:])
+            partial = held.tile([P, width], F32, name=f"partial{piece}")
+            x = held.tile([P, width], BF16, name=f"x{piece}")
+            nc.vector.tensor_tensor(partial[:], products[0][:], products[1][:], ADD)
+            nc.vector.tensor_tensor(x[:], partial[:], products[2][:], ADD)
+
+            for m in range(ROWS):
+                layer = layer_pool.tile([P, width], F32, name="layer")
+                nc.tensor.matmul(layer[:], w_by_row[:, m, :], x[:], start=True, stop=True)
+                result = held.tile([P, width], F32, name=f"result{m}_{piece}")
+                if m == 0 or piece < len(PIECES) - 1:
+                    nc.scalar.activation(result[:], layer[:], RELU, bias=bias[:, m : m + 1])
+                    nc.scalar.dma_start(out_by_partition[:, m, j], result[:])
+                else:
+                    nc.vector.tensor_scalar(result[:], layer[:], bias[:, m : m + 1], 0.0, ADD, MAX)
+                    nc.sync.dma_start(out_by_partition[:, m, j], result[:])
+            first += width

import concourse.mybir as mybir

BF16, F32, U16 = mybir.dt.bfloat16, mybir.dt.float32, mybir.dt.uint16
ADD, MULT, MAX = mybir.AluOpType.add, mybir.AluOpType.mult, mybir.AluOpType.max
RELU = mybir.ActivationFunctionType.Relu

P = 128
S = 2048
H = 256
V = 512
D = 3
M = 256
BANK = 512
FEATURES = H // P
ROWS = M // P
CHUNKS = S // BANK
PIECES = (V // 2, V // 4, V // 4)

FLOPS = 2 * P * H * S + 2 * P * M * V


def tile_lookup_pjmix_relu_kernel(tc, z, wt, u0, u1, u2, w, b, offs, out):
    nc = tc.nc
    with (
        tc.tile_pool(name="held", bufs=1) as held,
        tc.psum_pool(name="scratch", bufs=1) as scratch_pool,
        tc.psum_pool(name="projected", bufs=4) as projected_pool,
        tc.psum_pool(name="layer", bufs=3) as layer_pool,
    ):
        wt_tile = held.tile([P, FEATURES, P], BF16, name="wt_tile")
        z_tiles = [held.tile([P, FEATURES, BANK], BF16, name=f"z_tile{c}") for c in range(CHUNKS)]
        offsets = held.tile([P, D * V // 16], U16, name="offsets")
        u_tiles = [held.tile([P, V], F32, name=f"u_tile{d}") for d in range(D)]
        w_tile = held.tile([P, M], BF16, name="w_tile")
        bias = held.tile([P, ROWS], F32, name="bias")

        nc.sync.dma_start(wt_tile[:], wt.rearrange("(p k) r -> p k r", k=FEATURES))
        z_by_partition = z.rearrange("(p k) i -> p k i", k=FEATURES)
        for c, z_tile in enumerate(z_tiles):
            nc.sync.dma_start(z_tile[:], z_by_partition[:, :, c * BANK : (c + 1) * BANK])
        nc.sync.dma_start(offsets[:], offs)
        for u_tile, u in zip(u_tiles, (u0, u1, u2)):
            nc.sync.dma_start(u_tile[:], u)
        nc.sync.dma_start(w_tile[:], w)
        nc.sync.dma_start(bias[:], b.rearrange("(p m) o -> p (m o)", m=ROWS))

        zeros = held.tile([P, BANK], BF16, name="zeros")
        nc.vector.memset(zeros[:], 0.0)
        scratch = scratch_pool.tile([P, BANK], F32, name="scratch")
        for c in range(CHUNKS):
            nc.tensor.matmul(scratch[:], zeros[:, :P], zeros[:], start=True, stop=True)

        steps = [(c, 0, BANK) for c in range(CHUNKS - 1)]
        steps += [(CHUNKS - 1, 0, BANK // 2), (CHUNKS - 1, BANK // 2, BANK // 2)]
        table = held.tile([P, S], F32, name="table")
        for step, (c, start, width) in enumerate(steps):
            projected = projected_pool.tile([P, width], F32, name="projected")
            for k in range(FEATURES):
                nc.tensor.matmul(
                    projected[:],
                    wt_tile[:, k, :],
                    z_tiles[c][:, k, start : start + width],
                    start=k == 0,
                    stop=k == FEATURES - 1,
                )
            columns = table[:, c * BANK + start : c * BANK + start + width]
            if step % 2 == 0:
                nc.scalar.copy(columns, projected[:])
            else:
                nc.vector.tensor_copy(columns, projected[:])

        out_by_partition = out.rearrange("(p m) j -> p m j", m=ROWS)
        w_by_row = w_tile[:].rearrange("r (p m) -> r m p", m=ROWS)
        first = 0
        for piece, width in enumerate(PIECES):
            j = slice(first, first + width)

            products = []
            for d in range(D):
                entry = V * d + first
                listed = table[:].indirect(offsets[:, entry // 16 : (entry + width) // 16])
                product = held.tile([P, width], F32, name=f"product{d}_{piece}")
                nc.vector.tensor_tensor(product[:], listed, u_tiles[d][:, j], MULT)
                products.append(product)

            partial = held.tile([P, width], F32, name=f"partial{piece}")
            x = held.tile([P, width], BF16, name=f"x{piece}")
            nc.vector.tensor_tensor(partial[:], products[0][:], products[1][:], ADD)
            nc.vector.tensor_tensor(x[:], partial[:], products[2][:], ADD)

            for m in range(ROWS):
                layer = layer_pool.tile([P, width], F32, name="layer")
                nc.tensor.matmul(layer[:], w_by_row[:, m, :], x[:], start=True, stop=True)
                result = held.tile([P, width], F32, name=f"result{m}_{piece}")
                if m == 0 or piece < len(PIECES) - 1:
                    nc.scalar.activation(result[:], layer[:], RELU, bias=bias[:, m : m + 1])
                    nc.scalar.dma_start(out_by_partition[:, m, j], result[:])
                else:
                    nc.vector.tensor_scalar(result[:], layer[:], bias[:, m : m + 1], 0.0, ADD, MAX)
                    nc.sync.dma_start(out_by_partition[:, m, j], result[:])
            first += width
